import numpy as np
import ml_dtypes


def mxq(x, axis, fmt="e4m3"):
    dtype, down = {"e4m3": (ml_dtypes.float8_e4m3fn, 7), "e5m2": (ml_dtypes.float8_e5m2, 14)}[fmt]
    v = np.moveaxis(np.asarray(x, np.float32).astype(ml_dtypes.bfloat16).astype(np.float64), axis, -1)
    blocks = v.reshape(v.shape[:-1] + (-1, 32))
    amax = np.abs(blocks).max(-1, keepdims=True)
    byte = np.maximum(np.where(amax > 0, np.frexp(amax)[1] - 1 + 127, 0) - down, 1)
    scale = np.exp2(byte - 127.0)
    codes = (blocks / scale).astype(np.float32).astype(dtype).astype(np.float64)
    return np.moveaxis((codes * scale).reshape(v.shape), -1, axis)


WIDE = False


def mx_kscale(k):
    if not WIDE:
        return np.ones(k)
    levels = np.array([10, -10, 5, -5, 0])
    if k % 512:
        return np.exp2(np.random.permutation(np.resize(levels, k // 32))).repeat(32)
    a = np.empty((k // 512, 16))
    for p in range(k // 512):
        a[p, :8] = np.random.permutation(np.resize(levels, 8))
        for g in range(8):
            far = levels[np.abs(levels - a[p, g]) >= 10]
            a[p, g + 8] = far[np.random.randint(len(far))]
    return np.exp2(a.ravel()).repeat(32)


def f64(x):
    return np.asarray(x).astype(np.float64)


def striped(idx):
    return np.tile(idx.reshape(-1, 16).T, (8, 1)).astype(np.uint16)


def unstriped(offs):
    return offs[:16].T.reshape(-1).astype(np.int64)


def pack_weight(w):
    k, n = w.shape
    w = f64(np.asarray(w, np.float32).astype(ml_dtypes.bfloat16)).reshape(k // 32, 32, n)
    amax = np.abs(w).max(1)
    byte = np.clip(np.where(amax > 0, np.frexp(amax)[1] - 1 + 127 - 7, 1), 1, 254)
    scaled = (w * np.exp2(127.0 - byte)[:, None, :]).reshape(k, n).astype(np.float32)
    words = np.ascontiguousarray(scaled.reshape(k // 512, 128, 4, n).transpose(0, 1, 3, 2)).astype(ml_dtypes.float8_e4m3fn).view(np.uint8)
    return words, np.ascontiguousarray(byte.astype(np.uint8).reshape(k // 512, 16, n))


def unpack_weight(words, scales):
    g, p, n, _ = words.shape
    vals = np.ascontiguousarray(words).view(ml_dtypes.float8_e4m3fn).astype(np.float64) * np.repeat(np.exp2(scales.astype(np.float64) - 127.0), 8, axis=1)[..., None]
    return vals.transpose(0, 1, 3, 2).reshape(g * 512, n)


def silu(v):
    return v / (1.0 + np.exp(-np.maximum(v, -700.0)))


K, T, E, C, N = 1024, 1024, 16, 128, 256


def by_expert(wq, xq):
    return np.concatenate([wq[e].T @ xq[:, e * C:(e + 1) * C] for e in range(E)], axis=1)


def setup_inputs():
    n = np.random.standard_normal
    s = mx_kscale(K)[:, None]
    first = np.random.permutation(np.repeat(np.arange(E), T // E))
    second = (first + 1 + np.random.permutation(np.repeat(np.arange(E - 1), -(-T // (E - 1)))[:T])) % E
    while np.bincount(second, minlength=E).max() != T // E:
        load = np.bincount(second, minlength=E); hi, lo = int(load.argmax()), int(load.argmin())
        t = np.flatnonzero((second == hi) & (first != lo))[0]; second[t] = lo
    slot_token = np.empty(E * C, np.int64); pos = np.empty((2, T), np.int64); fill = np.zeros(E, np.int64)
    place = np.stack([np.random.permutation(C) for _ in range(E)])
    for r, deal in enumerate((first, second)):
        for t in np.random.permutation(T):
            e = deal[t]; j = e * C + place[e, fill[e]]; fill[e] += 1; slot_token[j] = t; pos[r, t] = j
    g = np.random.uniform(0.2, 0.8, T)
    packed = [pack_weight(m) for m in n((E, K, N)) / np.sqrt(K) / s[None]]
    return {
        "xT": (n((K, T)) * s).astype(np.float32),
        "w_words": np.stack([m[0] for m in packed]),
        "w_scales": np.stack([m[1] for m in packed]),
        "b": (0.3 * n((N, E))).astype(np.float32),
        "gate": np.stack([np.tile(g, (N, 1)), np.tile(1.0 - g, (N, 1))]).astype(np.float32),
        "offs": striped(slot_token),
        "pos1": striped(pos[0]),
        "pos2": striped(pos[1]),
    }


def reference(xT, w_words, w_scales, b, gate, offs, pos1, pos2):
    idx = unstriped(offs)
    xq = mxq(f64(xT)[:, idx], 0, "e4m3")
    w = np.stack([unpack_weight(w_words[e], w_scales[e]) for e in range(E)])
    y = by_expert(w, xq)
    y = silu(y + np.repeat(f64(b), C, axis=1))
    return f64(gate[0]) * y[:, unstriped(pos1)] + f64(gate[1]) * y[:, unstriped(pos2)]

@@ -1,0 +1,159 @@
+import concourse.masks as masks
+import concourse.mybir as mybir
+
+K, T, E, C, N = 1024, 1024, 16, 128, 256
+P = 128
+A = K // 512
+S = E * C
+H = N // P
+
+F32 = mybir.dt.float32
+BF16 = mybir.dt.bfloat16
+I32 = mybir.dt.int32
+U32 = mybir.dt.uint32
+U16 = mybir.dt.uint16
+U8 = mybir.dt.uint8
+FP8X4 = mybir.dt.float8_e4m3fn_x4
+SILU = mybir.ActivationFunctionType.Silu
+MULT = mybir.AluOpType.mult
+
+FLOPS = 2 * S * K * N
+
+CHUNKS = {0: (512, 256, 256), 1: (512, 512)}
+VSHARE = {0: (320, 160, 160), 1: (0, 0)}
+BLOCKS = {(a, sum(ws[:i])): (w, VSHARE[a][i]) for a, ws in CHUNKS.items() for i, w in enumerate(ws)}
+WORD_PIECES0 = (768, 768, 512)
+PIECES = (256, 512, 512, 512, 256)
+COMB = {0: (512, 512), 1: (512, 256, 256)}
+PE_ADD = {(0, 0), (0, 1), (1, 0)}
+
+
+def lay(dst, src, lo, hi):
+    return (dst[:, lo:hi, :].rearrange("p (c i) t -> p c t i", i=4),
+            src[:, :, lo:hi].rearrange("p t (c i) -> p c t i", i=4))
+
+
+def tile_routed_moe_kernel(tc, xT, w_words, w_scales, b, gate, offs, pos1, pos2, out):
+    nc = tc.nc
+    with (
+        tc.tile_pool(name="keep", bufs=1) as keep,
+        tc.psum_pool(name="psum", bufs=6) as psum,
+        tc.psum_pool(name="sums", bufs=2) as sums,
+    ):
+        offs_t = keep.tile([P, S // 16], U16, name="offs_t")
+        pos1_t = keep.tile([P, T // 16], U16, name="pos1_t")
+        pos2_t = keep.tile([P, T // 16], U16, name="pos2_t")
+        bias = keep.tile([P, H, E], F32, name="bias")
+        warm = keep.tile([P, 8], F32, name="warm")
+        raw = {(a, t): keep.tile([P, 4, w], F32, name=f"raw{a}_{t}") for (a, t), (w, v) in BLOCKS.items()}
+        grouped = {(a, t): keep.tile([P, w, 4], BF16, name=f"grouped{a}_{t}", align_bytes=64) for (a, t), (w, v) in BLOCKS.items()}
+        words = [keep.tile([P, T], U32, name=f"words{a}", align_bytes=64) for a in range(A)]
+        scales = keep.tile([P, T], U8, name="scales", align_bytes=64)
+        gwords = [keep.tile([P, S], U32, name=f"gwords{a}", align_bytes=64) for a in range(A)]
+        gscales = keep.tile([P, S], U8, name="gscales", align_bytes=64)
+        wsc = keep.tile([P, E, N], U8, name="wsc", align_bytes=64)
+        wt = [keep.tile([P, 2 * A, 4 * N], U8, name=f"wt{i}", align_bytes=64) for i in range(E // 2)]
+        y = [keep.tile([P, S], F32, name=f"y{h}") for h in range(H)]
+        gates = [[keep.tile([P, T], F32, name=f"gate{r}{h}") for h in range(H)] for r in range(2)]
+
+        ident = keep.tile([P, P], F32, name="ident")
+        nc.vector.memset(warm[:], 0.0)
+        nc.scalar.activation(warm[:, 0:1], warm[:, 1:2], SILU)
+        nc.gpsimd.memset(scales[:], 0)
+        masks.make_identity(nc, ident[:])
+        nc.vector.memset(wsc[:].bitcast(I32), 0)
+
+        def load_x(a, t):
+            rows = xT[512 * a : 512 * (a + 1), t : t + BLOCKS[a, t][0]]
+            nc.sync.dma_start(out=raw[a, t][:], in_=rows.rearrange("(p j) w -> p j w", j=4))
+
+        def load_scales(a):
+            for q in range(4):
+                nc.sync.dma_start(
+                    out=wsc[32 * q + 4 * a : 32 * q + 4 * a + 4, :, :].bitcast(I32),
+                    in_=w_scales[:, a, 4 * q : 4 * q + 4, :].rearrange("e i n -> i e n").bitcast(I32),
+                )
+
+        load_x(0, 0)
+        nc.sync.dma_start(offs_t[:], offs)
+        load_x(0, 512)
+        load_x(0, 768)
+        load_scales(0)
+        load_x(1, 0)
+        load_x(1, 512)
+        load_scales(1)
+        nc.sync.dma_start(out=bias[:], in_=b.rearrange("(h p) e -> p h e", p=P))
+        for i in range(E // 2):
+            nc.sync.dma_start(out=wt[i][:], in_=w_words[2 * i : 2 * i + 2].rearrange("e a p n r -> p (e a) (n r)"))
+        nc.sync.dma_start(pos1_t[:], pos1)
+        nc.sync.dma_start(pos2_t[:], pos2)
+        for h in range(H):
+            for r in range(2):
+                nc.sync.dma_start(out=gates[r][h][:], in_=gate[r, P * h : P * (h + 1), :])
+
+        def quantise(a, t):
+            w, v = BLOCKS[a, t]
+            if v:
+                d, s = lay(grouped[a, t], raw[a, t], 0, v)
+                nc.vector.tensor_copy(out=d, in_=s)
+            d, s = lay(grouped[a, t], raw[a, t], v, w)
+            nc.scalar.copy(out=d, in_=s)
+            cols = slice(t, t + w)
+            nc.vector.quantize_mx(
+                out=words[a][:, cols].bitcast(FP8X4),
+                scales=scales[4 * a :, cols],
+                in_=grouped[a, t][:].rearrange("p w j -> p (w j)"),
+            )
+
+        def gather(dst, src, lo, n):
+            nc.vector.tensor_copy(out=dst[:, lo : lo + n], in_=src[:].indirect(offs_t[:, lo // 16 : (lo + n) // 16]))
+
+        for t in (0, 512, 768):
+            quantise(0, t)
+        lo = 0
+        for n in WORD_PIECES0:
+            gather(gwords[0], words[0], lo, n)
+            lo += n
+        quantise(1, 0)
+        quantise(1, 512)
+
+        lo = 0
+        for n in PIECES:
+            gather(gscales, scales, lo, n)
+            gather(gwords[1], words[1], lo, n)
+            for e in range(lo // C, (lo + n) // C):
+                acc = psum.tile([P, H, C], F32, name="acc")
+                slots = slice(e * C, (e + 1) * C)
+                for h in range(H):
+                    for a in range(A):
+                        nc.tensor.matmul_mx(
+                            out=acc[:, h, :],
+                            lhsT=wt[e // 2][:, (e % 2) * A + a, 4 * P * h : 4 * P * (h + 1)].bitcast(FP8X4),
+                            lhsT_scale=wsc[4 * a :, e, P * h : P * (h + 1)],
+                            rhs=gwords[a][:, slots].bitcast(FP8X4),
+                            rhs_scale=gscales[4 * a :, slots],
+                            start=(a == 0),
+                            stop=(a == A - 1),
+                        )
+                    nc.scalar.activation(y[h][:, slots], acc[:, h, :], SILU, bias=bias[:, h, e : e + 1])
+            lo += n
+
+        for h in range(H):
+            lo = 0
+            for i, n in enumerate(COMB[h]):
+                cols = slice(lo, lo + n)
+                lists = slice(lo // 16, (lo + n) // 16)
+                m1 = keep.tile([P, n], F32, name=f"m1_{h}{i}")
+                m2 = keep.tile([P, n], F32, name=f"m2_{h}{i}")
+                o = keep.tile([P, n], F32, name=f"o_{h}{i}")
+                nc.vector.tensor_tensor(m1[:], y[h][:].indirect(pos1_t[:, lists]), gates[0][h][:, cols], MULT)
+                nc.vector.tensor_tensor(m2[:], y[h][:].indirect(pos2_t[:, lists]), gates[1][h][:, cols], MULT)
+                if (h, i) in PE_ADD:
+                    both = sums.tile([P, n], F32, name="both")
+                    nc.tensor.matmul(both[:], ident[:], m1[:], start=True, stop=False)
+                    nc.tensor.matmul(both[:], ident[:], m2[:], start=False, stop=True)
+                    nc.scalar.copy(out=o[:], in_=both[:])
+                else:
+                    nc.vector.tensor_add(o[:], m1[:], m2[:])
+                nc.sync.dma_start(out=out[P * h : P * (h + 1), cols], in_=o[:])
+                lo += n

@@ -19,9 +19,8 @@ MULT = mybir.AluOpType.mult
 
 FLOPS = 2 * S * K * N
 
-CHUNKS = {0: (512, 256, 256), 1: (512, 512)}
-VSHARE = {0: (320, 160, 160), 1: (0, 0)}
-BLOCKS = {(a, sum(ws[:i])): (w, VSHARE[a][i]) for a, ws in CHUNKS.items() for i, w in enumerate(ws)}
+CHUNKS = {(0, 0): (768, 448), (0, 768): (256, 160), (1, 0): (768, 0), (1, 768): (256, 160)}
+QUANT = {0: ((0, 512), (512, 256)), 768: ((768, 256),)}
 WORD_PIECES0 = (768, 768, 512)
 PIECES = (256, 512, 512, 512, 256)
 COMB = {0: (512, 512), 1: (512, 256, 256)}
@@ -45,8 +44,8 @@ def tile_routed_moe_kernel(tc, xT, w_words, w_scales, b, gate, offs, pos1, pos2,
         pos2_t = keep.tile([P, T // 16], U16, name="pos2_t")
         bias = keep.tile([P, H, E], F32, name="bias")
         warm = keep.tile([P, 8], F32, name="warm")
-        raw = {(a, t): keep.tile([P, 4, w], F32, name=f"raw{a}_{t}") for (a, t), (w, v) in BLOCKS.items()}
-        grouped = {(a, t): keep.tile([P, w, 4], BF16, name=f"grouped{a}_{t}", align_bytes=64) for (a, t), (w, v) in BLOCKS.items()}
+        raw = {(a, t): keep.tile([P, 4, w], F32, name=f"raw{a}_{t}") for (a, t), (w, v) in CHUNKS.items()}
+        grouped = {(a, t): keep.tile([P, w, 4], BF16, name=f"grouped{a}_{t}", align_bytes=64) for (a, t), (w, v) in CHUNKS.items()}
         words = [keep.tile([P, T], U32, name=f"words{a}", align_bytes=64) for a in range(A)]
         scales = keep.tile([P, T], U8, name="scales", align_bytes=64)
         gwords = [keep.tile([P, S], U32, name=f"gwords{a}", align_bytes=64) for a in range(A)]
@@ -64,7 +63,7 @@ def tile_routed_moe_kernel(tc, xT, w_words, w_scales, b, gate, offs, pos1, pos2,
         nc.vector.memset(wsc[:].bitcast(I32), 0)
 
         def load_x(a, t):
-            rows = xT[512 * a : 512 * (a + 1), t : t + BLOCKS[a, t][0]]
+            rows = xT[512 * a : 512 * (a + 1), t : t + CHUNKS[a, t][0]]
             nc.sync.dma_start(out=raw[a, t][:], in_=rows.rearrange("(p j) w -> p j w", j=4))
 
         def load_scales(a):
@@ -75,47 +74,54 @@ def tile_routed_moe_kernel(tc, xT, w_words, w_scales, b, gate, offs, pos1, pos2,
                 )
 
         load_x(0, 0)
-        nc.sync.dma_start(offs_t[:], offs)
-        load_x(0, 512)
         load_x(0, 768)
-        load_scales(0)
+        nc.sync.dma_start(offs_t[:], offs)
         load_x(1, 0)
-        load_x(1, 512)
+        load_x(1, 768)
+        load_scales(0)
         load_scales(1)
-        nc.sync.dma_start(out=bias[:], in_=b.rearrange("(h p) e -> p h e", p=P))
         for i in range(E // 2):
             nc.sync.dma_start(out=wt[i][:], in_=w_words[2 * i : 2 * i + 2].rearrange("e a p n r -> p (e a) (n r)"))
+            if i == 0:
+                nc.sync.dma_start(out=bias[:], in_=b.rearrange("(h p) e -> p h e", p=P))
         nc.sync.dma_start(pos1_t[:], pos1)
         nc.sync.dma_start(pos2_t[:], pos2)
         for h in range(H):
             for r in range(2):
                 nc.sync.dma_start(out=gates[r][h][:], in_=gate[r, P * h : P * (h + 1), :])
 
-        def quantise(a, t):
-            w, v = BLOCKS[a, t]
+        def interleave(a, t):
+            w, v = CHUNKS[a, t]
             if v:
                 d, s = lay(grouped[a, t], raw[a, t], 0, v)
                 nc.vector.tensor_copy(out=d, in_=s)
             d, s = lay(grouped[a, t], raw[a, t], v, w)
             nc.scalar.copy(out=d, in_=s)
-            cols = slice(t, t + w)
-            nc.vector.quantize_mx(
-                out=words[a][:, cols].bitcast(FP8X4),
-                scales=scales[4 * a :, cols],
-                in_=grouped[a, t][:].rearrange("p w j -> p (w j)"),
-            )
+
+        def quantise(a, t):
+            for lo, n in QUANT[t]:
+                cols = slice(lo, lo + n)
+                nc.vector.quantize_mx(
+                    out=words[a][:, cols].bitcast(FP8X4),
+                    scales=scales[4 * a :, cols],
+                    in_=grouped[a, t][:, lo - t : lo - t + n, :].rearrange("p w j -> p (w j)"),
+                )
 
         def gather(dst, src, lo, n):
             nc.vector.tensor_copy(out=dst[:, lo : lo + n], in_=src[:].indirect(offs_t[:, lo // 16 : (lo + n) // 16]))
 
-        for t in (0, 512, 768):
-            quantise(0, t)
+        interleave(0, 0)
+        quantise(0, 0)
+        interleave(0, 768)
+        quantise(0, 768)
         lo = 0
         for n in WORD_PIECES0:
             gather(gwords[0], words[0], lo, n)
             lo += n
+        interleave(1, 0)
+        interleave(1, 768)
         quantise(1, 0)
-        quantise(1, 512)
+        quantise(1, 768)
 
         lo = 0
         for n in PIECES:
@@ -138,6 +144,19 @@ def tile_routed_moe_kernel(tc, xT, w_words, w_scales, b, gate, offs, pos1, pos2,
                     nc.scalar.activation(y[h][:, slots], acc[:, h, :], SILU, bias=bias[:, h, e : e + 1])
             lo += n
 
+        late = []
+
+        def finish(h, i, lo, n, m1, m2):
+            o = keep.tile([P, n], F32, name=f"o_{h}{i}")
+            if (h, i) in PE_ADD:
+                both = sums.tile([P, n], F32, name="both")
+                nc.tensor.matmul(both[:], ident[:], m1[:], start=True, stop=False)
+                nc.tensor.matmul(both[:], ident[:], m2[:], start=False, stop=True)
+                nc.scalar.copy(out=o[:], in_=both[:])
+            else:
+                nc.vector.tensor_add(o[:], m1[:], m2[:])
+            nc.sync.dma_start(out=out[P * h : P * (h + 1), lo : lo + n], in_=o[:])
+
         for h in range(H):
             lo = 0
             for i, n in enumerate(COMB[h]):
@@ -145,15 +164,10 @@ def tile_routed_moe_kernel(tc, xT, w_words, w_scales, b, gate, offs, pos1, pos2,
                 lists = slice(lo // 16, (lo + n) // 16)
                 m1 = keep.tile([P, n], F32, name=f"m1_{h}{i}")
                 m2 = keep.tile([P, n], F32, name=f"m2_{h}{i}")
-                o = keep.tile([P, n], F32, name=f"o_{h}{i}")
                 nc.vector.tensor_tensor(m1[:], y[h][:].indirect(pos1_t[:, lists]), gates[0][h][:, cols], MULT)
+                for args in late:
+                    finish(*args)
                 nc.vector.tensor_tensor(m2[:], y[h][:].indirect(pos2_t[:, lists]), gates[1][h][:, cols], MULT)
-                if (h, i) in PE_ADD:
-                    both = sums.tile([P, n], F32, name="both")
-                    nc.tensor.matmul(both[:], ident[:], m1[:], start=True, stop=False)
-                    nc.tensor.matmul(both[:], ident[:], m2[:], start=False, stop=True)
-                    nc.scalar.copy(out=o[:], in_=both[:])
-                else:
-                    nc.vector.tensor_add(o[:], m1[:], m2[:])
-                nc.sync.dma_start(out=out[P * h : P * (h + 1), cols], in_=o[:])
+                late = [(h, i, lo, n, m1, m2)]
                 lo += n
+        finish(*late[0])

@@ -19,9 +19,11 @@ MULT = mybir.AluOpType.mult
 
 FLOPS = 2 * S * K * N
 
-CHUNKS = {(0, 0): (768, 448), (0, 768): (256, 160), (1, 0): (768, 0), (1, 768): (256, 160)}
+CHUNKS = {(0, 0): (768, 448), (0, 768): (256, 160), (1, 0): (768, 96), (1, 768): (256, 160)}
 QUANT = {0: ((0, 512), (512, 256)), 768: ((768, 256),)}
 WORD_PIECES0 = (768, 768, 512)
+WHOLE = 8
+GATE = 512
 PIECES = (256, 512, 512, 512, 256)
 COMB = {0: (512, 512), 1: (512, 256, 256)}
 PE_ADD = {(0, 0), (0, 1), (1, 0)}
@@ -51,9 +53,10 @@ def tile_routed_moe_kernel(tc, xT, w_words, w_scales, b, gate, offs, pos1, pos2,
         gwords = [keep.tile([P, S], U32, name=f"gwords{a}", align_bytes=64) for a in range(A)]
         gscales = keep.tile([P, S], U8, name="gscales", align_bytes=64)
         wsc = keep.tile([P, E, N], U8, name="wsc", align_bytes=64)
-        wt = [keep.tile([P, 2 * A, 4 * N], U8, name=f"wt{i}", align_bytes=64) for i in range(E // 2)]
+        whole = [keep.tile([P, 2 * A, 4 * N], U8, name=f"whole{i}", align_bytes=64) for i in range(WHOLE // 2)]
+        half = [[keep.tile([P, 4 * A, 4 * P], U8, name=f"half{h}{i}", align_bytes=64) for i in range((E - WHOLE) // 4)] for h in range(H)]
         y = [keep.tile([P, S], F32, name=f"y{h}") for h in range(H)]
-        gates = [[keep.tile([P, T], F32, name=f"gate{r}{h}") for h in range(H)] for r in range(2)]
+        gates = [[[keep.tile([P, GATE], F32, name=f"gate{r}{h}{g}") for g in range(2)] for h in range(H)] for r in range(2)]
 
         ident = keep.tile([P, P], F32, name="ident")
         nc.vector.memset(warm[:], 0.0)
@@ -80,15 +83,22 @@ def tile_routed_moe_kernel(tc, xT, w_words, w_scales, b, gate, offs, pos1, pos2,
         load_x(1, 768)
         load_scales(0)
         load_scales(1)
-        for i in range(E // 2):
-            nc.sync.dma_start(out=wt[i][:], in_=w_words[2 * i : 2 * i + 2].rearrange("e a p n r -> p (e a) (n r)"))
+        for i in range(WHOLE // 2):
+            nc.sync.dma_start(out=whole[i][:], in_=w_words[2 * i : 2 * i + 2].rearrange("e a p n r -> p (e a) (n r)"))
             if i == 0:
                 nc.sync.dma_start(out=bias[:], in_=b.rearrange("(h p) e -> p h e", p=P))
         nc.sync.dma_start(pos1_t[:], pos1)
         nc.sync.dma_start(pos2_t[:], pos2)
         for h in range(H):
-            for r in range(2):
-                nc.sync.dma_start(out=gates[r][h][:], in_=gate[r, P * h : P * (h + 1), :])
+            for i in range((E - WHOLE) // 4):
+                e = WHOLE + 4 * i
+                nc.sync.dma_start(
+                    out=half[h][i][:],
+                    in_=w_words[e : e + 4, :, :, P * h : P * (h + 1), :].rearrange("e a p n r -> p (e a) (n r)"),
+                )
+            for g in range(2):
+                for r in range(2):
+                    nc.sync.dma_start(out=gates[r][h][g][:], in_=gate[r, P * h : P * (h + 1), GATE * g : GATE * (g + 1)])
 
         def interleave(a, t):
             w, v = CHUNKS[a, t]
@@ -123,26 +133,37 @@ def tile_routed_moe_kernel(tc, xT, w_words, w_scales, b, gate, offs, pos1, pos2,
         quantise(1, 0)
         quantise(1, 768)
 
+        def expert(e, h):
+            acc = psum.tile([P, C], F32, name="acc")
+            slots = slice(e * C, (e + 1) * C)
+            for a in range(A):
+                if e < WHOLE:
+                    codes = whole[e // 2][:, (e % 2) * A + a, 4 * P * h : 4 * P * (h + 1)]
+                else:
+                    codes = half[h][(e - WHOLE) // 4][:, (e % 4) * A + a, :]
+                nc.tensor.matmul_mx(
+                    out=acc[:],
+                    lhsT=codes.bitcast(FP8X4),
+                    lhsT_scale=wsc[4 * a :, e, P * h : P * (h + 1)],
+                    rhs=gwords[a][:, slots].bitcast(FP8X4),
+                    rhs_scale=gscales[4 * a :, slots],
+                    start=(a == 0),
+                    stop=(a == A - 1),
+                )
+            nc.scalar.activation(y[h][:, slots], acc[:], SILU, bias=bias[:, h, e : e + 1])
+
         lo = 0
         for n in PIECES:
             gather(gscales, scales, lo, n)
             gather(gwords[1], words[1], lo, n)
             for e in range(lo // C, (lo + n) // C):
-                acc = psum.tile([P, H, C], F32, name="acc")
-                slots = slice(e * C, (e + 1) * C)
-                for h in range(H):
-                    for a in range(A):
-                        nc.tensor.matmul_mx(
-                            out=acc[:, h, :],
-                            lhsT=wt[e // 2][:, (e % 2) * A + a, 4 * P * h : 4 * P * (h + 1)].bitcast(FP8X4),
-                            lhsT_scale=wsc[4 * a :, e, P * h : P * (h + 1)],
-                            rhs=gwords[a][:, slots].bitcast(FP8X4),
-                            rhs_scale=gscales[4 * a :, slots],
-                            start=(a == 0),
-                            stop=(a == A - 1),
-                        )
-                    nc.scalar.activation(y[h][:, slots], acc[:, h, :], SILU, bias=bias[:, h, e : e + 1])
+                expert(e, 0)
+                if e < WHOLE:
+                    expert(e, 1)
             lo += n
+
+        for e in range(WHOLE, E):
+            expert(e, 1)
 
         late = []
 
@@ -160,14 +181,13 @@ def tile_routed_moe_kernel(tc, xT, w_words, w_scales, b, gate, offs, pos1, pos2,
         for h in range(H):
             lo = 0
             for i, n in enumerate(COMB[h]):
-                cols = slice(lo, lo + n)
                 lists = slice(lo // 16, (lo + n) // 16)
                 m1 = keep.tile([P, n], F32, name=f"m1_{h}{i}")
                 m2 = keep.tile([P, n], F32, name=f"m2_{h}{i}")
-                nc.vector.tensor_tensor(m1[:], y[h][:].indirect(pos1_t[:, lists]), gates[0][h][:, cols], MULT)
+                nc.vector.tensor_tensor(m1[:], y[h][:].indirect(pos1_t[:, lists]), gates[0][h][lo // GATE][:, lo % GATE : lo % GATE + n], MULT)
                 for args in late:
                     finish(*args)
-                nc.vector.tensor_tensor(m2[:], y[h][:].indirect(pos2_t[:, lists]), gates[1][h][:, cols], MULT)
+                nc.vector.tensor_tensor(m2[:], y[h][:].indirect(pos2_t[:, lists]), gates[1][h][lo // GATE][:, lo % GATE : lo % GATE + n], MULT)
                 late = [(h, i, lo, n, m1, m2)]
                 lo += n
         finish(*late[0])

@@ -25,8 +25,8 @@ WORD_PIECES0 = (768, 768, 512)
 WHOLE = 8
 GATE = 512
 PIECES = (256, 512, 512, 512, 256)
-COMB = {0: (512, 512), 1: (512, 256, 256)}
-PE_ADD = {(0, 0), (0, 1), (1, 0)}
+COMB = {0: (512, 512), 1: (512, 384, 128)}
+PE_ADD = {(1, 0)}
 
 
 def lay(dst, src, lo, hi):
@@ -69,23 +69,23 @@ def tile_routed_moe_kernel(tc, xT, w_words, w_scales, b, gate, offs, pos1, pos2,
             rows = xT[512 * a : 512 * (a + 1), t : t + CHUNKS[a, t][0]]
             nc.sync.dma_start(out=raw[a, t][:], in_=rows.rearrange("(p j) w -> p j w", j=4))
 
-        def load_scales(a):
-            for q in range(4):
-                nc.sync.dma_start(
-                    out=wsc[32 * q + 4 * a : 32 * q + 4 * a + 4, :, :].bitcast(I32),
-                    in_=w_scales[:, a, 4 * q : 4 * q + 4, :].rearrange("e i n -> i e n").bitcast(I32),
-                )
+        def load_scales(a, i):
+            nc.sync.dma_start(
+                out=wsc[4 * a + i : P : 32, :, :].bitcast(I32),
+                in_=w_scales[:, a, i : 16 : 4, :].rearrange("e q n -> q e n").bitcast(I32),
+            )
 
         load_x(0, 0)
         load_x(0, 768)
         nc.sync.dma_start(offs_t[:], offs)
         load_x(1, 0)
         load_x(1, 768)
-        load_scales(0)
-        load_scales(1)
+        rows = [(a, i) for a in range(A) for i in range(4)]
         for i in range(WHOLE // 2):
             nc.sync.dma_start(out=whole[i][:], in_=w_words[2 * i : 2 * i + 2].rearrange("e a p n r -> p (e a) (n r)"))
-            if i == 0:
+            for a, q in rows[3 * i : 3 * i + 3]:
+                load_scales(a, q)
+            if i == 2:
                 nc.sync.dma_start(out=bias[:], in_=b.rearrange("(h p) e -> p h e", p=P))
         nc.sync.dma_start(pos1_t[:], pos1)
         nc.sync.dma_start(pos2_t[:], pos2)

import concourse.masks as masks
import concourse.mybir as mybir

K, T, E, C, N = 1024, 1024, 16, 128, 256
P = 128
A = K // 512
S = E * C
H = N // P

F32 = mybir.dt.float32
BF16 = mybir.dt.bfloat16
I32 = mybir.dt.int32
U32 = mybir.dt.uint32
U16 = mybir.dt.uint16
U8 = mybir.dt.uint8
FP8X4 = mybir.dt.float8_e4m3fn_x4
SILU = mybir.ActivationFunctionType.Silu
MULT = mybir.AluOpType.mult

FLOPS = 2 * S * K * N

CHUNKS = {(0, 0): (768, 448), (0, 768): (256, 160), (1, 0): (768, 96), (1, 768): (256, 160)}
QUANT = {0: ((0, 512), (512, 256)), 768: ((768, 256),)}
WORD_PIECES0 = (768, 768, 512)
WHOLE = 8
GATE = 512
PIECES = (256, 512, 512, 512, 256)
COMB = {0: (512, 512), 1: (512, 384, 128)}
PE_ADD = {(1, 0)}


def lay(dst, src, lo, hi):
    return (dst[:, lo:hi, :].rearrange("p (c i) t -> p c t i", i=4),
            src[:, :, lo:hi].rearrange("p t (c i) -> p c t i", i=4))


def tile_routed_moe_kernel(tc, xT, w_words, w_scales, b, gate, offs, pos1, pos2, out):
    nc = tc.nc
    with (
        tc.tile_pool(name="keep", bufs=1) as keep,
        tc.psum_pool(name="psum", bufs=6) as psum,
        tc.psum_pool(name="sums", bufs=2) as sums,
    ):
        offs_t = keep.tile([P, S // 16], U16, name="offs_t")
        pos1_t = keep.tile([P, T // 16], U16, name="pos1_t")
        pos2_t = keep.tile([P, T // 16], U16, name="pos2_t")
        bias = keep.tile([P, H, E], F32, name="bias")
        warm = keep.tile([P, 8], F32, name="warm")
        raw = {(a, t): keep.tile([P, 4, w], F32, name=f"raw{a}_{t}") for (a, t), (w, v) in CHUNKS.items()}
        grouped = {(a, t): keep.tile([P, w, 4], BF16, name=f"grouped{a}_{t}", align_bytes=64) for (a, t), (w, v) in CHUNKS.items()}
        words = [keep.tile([P, T], U32, name=f"words{a}", align_bytes=64) for a in range(A)]
        scales = keep.tile([P, T], U8, name="scales", align_bytes=64)
        gwords = [keep.tile([P, S], U32, name=f"gwords{a}", align_bytes=64) for a in range(A)]
        gscales = keep.tile([P, S], U8, name="gscales", align_bytes=64)
        wsc = keep.tile([P, E, N], U8, name="wsc", align_bytes=64)
        whole = [keep.tile([P, 2 * A, 4 * N], U8, name=f"whole{i}", align_bytes=64) for i in range(WHOLE // 2)]
        half = [[keep.tile([P, 4 * A, 4 * P], U8, name=f"half{h}{i}", align_bytes=64) for i in range((E - WHOLE) // 4)] for h in range(H)]
        y = [keep.tile([P, S], F32, name=f"y{h}") for h in range(H)]
        gates = [[[keep.tile([P, GATE], F32, name=f"gate{r}{h}{g}") for g in range(2)] for h in range(H)] for r in range(2)]

        ident = keep.tile([P, P], F32, name="ident")
        nc.vector.memset(warm[:], 0.0)
        nc.scalar.activation(warm[:, 0:1], warm[:, 1:2], SILU)
        nc.gpsimd.memset(scales[:], 0)
        masks.make_identity(nc, ident[:])
        nc.vector.memset(wsc[:].bitcast(I32), 0)

        def load_x(a, t):
            rows = xT[512 * a : 512 * (a + 1), t : t + CHUNKS[a, t][0]]
            nc.sync.dma_start(out=raw[a, t][:], in_=rows.rearrange("(p j) w -> p j w", j=4))

        def load_scales(a, i):
            nc.sync.dma_start(
                out=wsc[4 * a + i : P : 32, :, :].bitcast(I32),
                in_=w_scales[:, a, i : 16 : 4, :].rearrange("e q n -> q e n").bitcast(I32),
            )

        load_x(0, 0)
        load_x(0, 768)
        nc.sync.dma_start(offs_t[:], offs)
        load_x(1, 0)
        load_x(1, 768)
        rows = [(a, i) for a in range(A) for i in range(4)]
        for i in range(WHOLE // 2):
            nc.sync.dma_start(out=whole[i][:], in_=w_words[2 * i : 2 * i + 2].rearrange("e a p n r -> p (e a) (n r)"))
            for a, q in rows[3 * i : 3 * i + 3]:
                load_scales(a, q)
            if i == 2:
                nc.sync.dma_start(out=bias[:], in_=b.rearrange("(h p) e -> p h e", p=P))
        nc.sync.dma_start(pos1_t[:], pos1)
        nc.sync.dma_start(pos2_t[:], pos2)
        for h in range(H):
            for i in range((E - WHOLE) // 4):
                e = WHOLE + 4 * i
                nc.sync.dma_start(
                    out=half[h][i][:],
                    in_=w_words[e : e + 4, :, :, P * h : P * (h + 1), :].rearrange("e a p n r -> p (e a) (n r)"),
                )
            for g in range(2):
                for r in range(2):
                    nc.sync.dma_start(out=gates[r][h][g][:], in_=gate[r, P * h : P * (h + 1), GATE * g : GATE * (g + 1)])

        def interleave(a, t):
            w, v = CHUNKS[a, t]
            if v:
                d, s = lay(grouped[a, t], raw[a, t], 0, v)
                nc.vector.tensor_copy(out=d, in_=s)
            d, s = lay(grouped[a, t], raw[a, t], v, w)
            nc.scalar.copy(out=d, in_=s)

        def quantise(a, t):
            for lo, n in QUANT[t]:
                cols = slice(lo, lo + n)
                nc.vector.quantize_mx(
                    out=words[a][:, cols].bitcast(FP8X4),
                    scales=scales[4 * a :, cols],
                    in_=grouped[a, t][:, lo - t : lo - t + n, :].rearrange("p w j -> p (w j)"),
                )

        def gather(dst, src, lo, n):
            nc.vector.tensor_copy(out=dst[:, lo : lo + n], in_=src[:].indirect(offs_t[:, lo // 16 : (lo + n) // 16]))

        interleave(0, 0)
        quantise(0, 0)
        interleave(0, 768)
        quantise(0, 768)
        lo = 0
        for n in WORD_PIECES0:
            gather(gwords[0], words[0], lo, n)
            lo += n
        interleave(1, 0)
        interleave(1, 768)
        quantise(1, 0)
        quantise(1, 768)

        def expert(e, h):
            acc = psum.tile([P, C], F32, name="acc")
            slots = slice(e * C, (e + 1) * C)
            for a in range(A):
                if e < WHOLE:
                    codes = whole[e // 2][:, (e % 2) * A + a, 4 * P * h : 4 * P * (h + 1)]
                else:
                    codes = half[h][(e - WHOLE) // 4][:, (e % 4) * A + a, :]
                nc.tensor.matmul_mx(
                    out=acc[:],
                    lhsT=codes.bitcast(FP8X4),
                    lhsT_scale=wsc[4 * a :, e, P * h : P * (h + 1)],
                    rhs=gwords[a][:, slots].bitcast(FP8X4),
                    rhs_scale=gscales[4 * a :, slots],
                    start=(a == 0),
                    stop=(a == A - 1),
                )
            nc.scalar.activation(y[h][:, slots], acc[:], SILU, bias=bias[:, h, e : e + 1])

        lo = 0
        for n in PIECES:
            gather(gscales, scales, lo, n)
            gather(gwords[1], words[1], lo, n)
            for e in range(lo // C, (lo + n) // C):
                expert(e, 0)
                if e < WHOLE:
                    expert(e, 1)
            lo += n

        for e in range(WHOLE, E):
            expert(e, 1)

        late = []

        def finish(h, i, lo, n, m1, m2):
            o = keep.tile([P, n], F32, name=f"o_{h}{i}")
            if (h, i) in PE_ADD:
                both = sums.tile([P, n], F32, name="both")
                nc.tensor.matmul(both[:], ident[:], m1[:], start=True, stop=False)
                nc.tensor.matmul(both[:], ident[:], m2[:], start=False, stop=True)
                nc.scalar.copy(out=o[:], in_=both[:])
            else:
                nc.vector.tensor_add(o[:], m1[:], m2[:])
            nc.sync.dma_start(out=out[P * h : P * (h + 1), lo : lo + n], in_=o[:])

        for h in range(H):
            lo = 0
            for i, n in enumerate(COMB[h]):
                lists = slice(lo // 16, (lo + n) // 16)
                m1 = keep.tile([P, n], F32, name=f"m1_{h}{i}")
                m2 = keep.tile([P, n], F32, name=f"m2_{h}{i}")
                nc.vector.tensor_tensor(m1[:], y[h][:].indirect(pos1_t[:, lists]), gates[0][h][lo // GATE][:, lo % GATE : lo % GATE + n], MULT)
                for args in late:
                    finish(*args)
                nc.vector.tensor_tensor(m2[:], y[h][:].indirect(pos2_t[:, lists]), gates[1][h][lo // GATE][:, lo % GATE : lo % GATE + n], MULT)
                late = [(h, i, lo, n, m1, m2)]
                lo += n
        finish(*late[0])
